import numpy as np
import ml_dtypes


def mxq(x, axis, fmt="e4m3"):
    dtype, down = {"e4m3": (ml_dtypes.float8_e4m3fn, 7), "e5m2": (ml_dtypes.float8_e5m2, 14)}[fmt]
    v = np.moveaxis(np.asarray(x, np.float32).astype(ml_dtypes.bfloat16).astype(np.float64), axis, -1)
    blocks = v.reshape(v.shape[:-1] + (-1, 32))
    amax = np.abs(blocks).max(-1, keepdims=True)
    byte = np.maximum(np.where(amax > 0, np.frexp(amax)[1] - 1 + 127, 0) - down, 1)
    scale = np.exp2(byte - 127.0)
    codes = (blocks / scale).astype(np.float32).astype(dtype).astype(np.float64)
    return np.moveaxis((codes * scale).reshape(v.shape), -1, axis)


WIDE = False


def mx_kscale(k):
    if not WIDE:
        return np.ones(k)
    levels = np.array([10, -10, 5, -5, 0])
    if k % 512:
        return np.exp2(np.random.permutation(np.resize(levels, k // 32))).repeat(32)
    a = np.empty((k // 512, 16))
    for p in range(k // 512):
        a[p, :8] = np.random.permutation(np.resize(levels, 8))
        for g in range(8):
            far = levels[np.abs(levels - a[p, g]) >= 10]
            a[p, g + 8] = far[np.random.randint(len(far))]
    return np.exp2(a.ravel()).repeat(32)


def f64(x):
    return np.asarray(x).astype(np.float64)


def striped(idx):
    return np.tile(idx.reshape(-1, 16).T, (8, 1)).astype(np.uint16)


def unstriped(offs):
    return offs[:16].T.reshape(-1).astype(np.int64)


E2M1 = np.array([0.0, 0.5, 1.0, 1.5, 2.0, 3.0, 4.0, 6.0, -0.0, -0.5, -1.0, -1.5, -2.0, -3.0, -4.0, -6.0])


def pack_weight(w, fmt):
    k, n = w.shape
    w = f64(np.asarray(w, np.float32).astype(ml_dtypes.bfloat16)).reshape(k // 32, 32, n)
    amax = np.abs(w).max(1)
    if fmt == "e4m3":
        byte = np.frexp(amax)[1] - 1 + 127 - 7
    else:
        mant, ex = np.frexp(amax / 6.0)
        byte = np.where(mant > 0.5, ex, ex - 1) + 127
    byte = np.clip(np.where(amax > 0, byte, 1), 1, 254)
    scaled = (w * np.exp2(127.0 - byte)[:, None, :]).reshape(k, n).astype(np.float32)
    by_word = np.ascontiguousarray(scaled.reshape(k // 512, 128, 4, n).transpose(0, 1, 3, 2))
    if fmt == "e4m3":
        words = by_word.astype(ml_dtypes.float8_e4m3fn).view(np.uint8)
    else:
        c = by_word.astype(ml_dtypes.float4_e2m1fn).view(np.uint8) & 0xF
        words = (c[..., 0::2] | (c[..., 1::2] << 4)).reshape(k // 512, 128, 2 * n)
    return np.ascontiguousarray(words), np.ascontiguousarray(byte.astype(np.uint8).reshape(k // 512, 16, n))


def unpack_weight(words, scales, fmt):
    g, _, n = scales.shape
    words = np.ascontiguousarray(words).reshape(g, 128, n, -1)
    if fmt == "e4m3":
        vals = words.view(ml_dtypes.float8_e4m3fn).astype(np.float64)
    else:
        nib = np.empty((g, 128, n, 4), np.uint8)
        nib[..., 0::2] = words & 0xF
        nib[..., 1::2] = words >> 4
        vals = E2M1[nib]
    vals = vals * np.repeat(np.exp2(scales.astype(np.float64) - 127.0), 8, axis=1)[..., None]
    return vals.transpose(0, 1, 3, 2).reshape(g * 512, n)


def gelu(v):
    return 0.5 * v * (1.0 + np.tanh(np.sqrt(2.0 / np.pi) * (v + 0.044715 * v**3)))


K, T, S, S2 = 1024, 4096, 1024, 512

def setup_inputs():
    n = np.random.standard_normal
    s = mx_kscale(K)[:, None]
    d = {}
    d["tab_words"], d["tab_scales"] = pack_weight(0.2 * n((K, T)) * s, "e4m3")
    d["offs"] = striped(np.random.permutation(T)[:S])
    d["offs2"] = striped(np.random.permutation(T)[:S2])
    d["w4_words"], d["w4_scales"] = pack_weight(5.6 / K**0.5 * n((K, K)) / s, "e2m1")
    d["w1"] = (5.6 / K**0.5 * n((K, K)) / s).astype(np.float32)
    d["gain"] = (4.3 / K**0.5 * np.exp(0.3 * n(K)) / s[:, 0]).astype(np.float32)
    d["phase"] = np.random.uniform(-0.9, 0.9, S2).astype(np.float32)
    d["loss"] = np.exp(0.5 * n((S2, S))).astype(np.float32)
    return d

def reference(tab_words, tab_scales, offs, offs2, w4_words, w4_scales, w1, gain, phase, loss):
    TW = unpack_weight(tab_words, tab_scales, "e4m3")
    v = TW[:, unstriped(offs)]
    v2 = TW[:, unstriped(offs2)]
    W4 = unpack_weight(w4_words, w4_scales, "e2m1")
    w1q = mxq(f64(w1), 0, "e4m3")
    x = W4.T @ v + w1q.T @ v
    h = np.exp(-np.abs(x)) * f64(gain)[:, None]
    hq = mxq(h, 0, "e4m3")
    e = v2.T @ hq
    beat = np.cos(e + f64(phase)[:, None])
    return beat * f64(loss)

@@ -1,0 +1,291 @@
+import math
+from contextlib import ExitStack
+
+import concourse.mybir as mybir
+
+K, T, S, S2 = 1024, 4096, 1024, 512
+FLOPS = 2 * (2 * K * K * S + K * S * S2)
+
+F32 = mybir.dt.float32
+BF16 = mybir.dt.bfloat16
+I32 = mybir.dt.int32
+U32 = mybir.dt.uint32
+U16 = mybir.dt.uint16
+U8 = mybir.dt.uint8
+FP8X4 = mybir.dt.float8_e4m3fn_x4
+FP4X4 = mybir.dt.float4_e2m1fn_x4
+ALU = mybir.AluOpType
+ACT = mybir.ActivationFunctionType
+
+P = 128
+PACK = 4
+PASS = P * PACK
+PASSES = K // PASS
+NJ = 512
+HALVES = S // NJ
+MT = S2 // P
+TWO_PI = 2.0 * math.pi
+W1_SLOT = {(0, 0): "slot_w00", (1, 0): "slot_w10", (0, 1): "slot_w01", (1, 1): "slot_w4"}
+
+
+def tile_list_beat_disturbance_scores_kernel(
+    tc, tab_words, tab_scales, offs, offs2, w4_words, w4_scales, w1, gain, phase, loss, out
+):
+    nc = tc.nc
+    with ExitStack() as ctx:
+        held = ctx.enter_context(tc.tile_pool(name="held", bufs=1))
+        ring = ctx.enter_context(tc.tile_pool(name="ring", bufs=2))
+        psum = ctx.enter_context(tc.psum_pool(name="psum", bufs=1))
+
+        def keep(name, shape, dtype, tag=None):
+            return held.tile(shape, dtype, name=name, tag=tag or name, align_bytes=64)
+
+        tab_planes = keep("tab_planes", [P, T], U8, "slot_w01")
+        v_planes_hi = keep("v_planes_hi", [P, S], U8)
+        warm = keep("warm", [P, 16], F32, "slot_tab0")
+        nc.vector.memset(warm[:, 0:8], 0.0)
+        nc.vector.memset(tab_planes[:].bitcast(I32), 0)
+        nc.vector.memset(v_planes_hi[:].bitcast(I32), 0)
+        nc.scalar.activation(warm[:, 8:9], warm[:, 0:1], ACT.Exp)
+
+        list1 = keep("list1", [P, S // 16], U16)
+        list2 = keep("list2", [P, S2 // 16], U16)
+        w4_raw = keep("w4_raw", [P, PASSES * 2 * K], U8, "slot_w4")
+        tab = {}
+        w1_raw = {}
+
+        def load_tab(a):
+            tab[a] = keep("tab%d" % a, [P, T], I32, ("slot_tab0", "slot_w00")[a])
+            nc.sync.dma_start(out=tab[a][:], in_=tab_words[a].rearrange("p t i -> p (t i)").bitcast(I32))
+
+        def load_w1(a, b):
+            w1_raw[a, b] = keep("w1_raw%d%d" % (a, b), [P, PACK, PASS], F32, W1_SLOT[a, b])
+            rows = w1[PASS * a : PASS * (a + 1), PASS * b : PASS * (b + 1)]
+            nc.sync.dma_start(out=w1_raw[a, b][:], in_=rows.rearrange("(p j) c -> p j c", j=PACK))
+
+        nc.sync.dma_start(list1[:], offs)
+        nc.sync.dma_start(
+            out=w4_raw[:].bitcast(I32).rearrange("p (a c) -> p a c", a=PASSES),
+            in_=w4_words.bitcast(I32).rearrange("a p c -> p a c"),
+        )
+        load_w1(0, 0)
+        load_w1(1, 0)
+        nc.sync.dma_start(list2[:], offs2)
+        for q in range(4):
+            nc.scalar.dma_start(
+                out=tab_planes[32 * q : 32 * q + 8, :].bitcast(I32),
+                in_=tab_scales[:, 4 * q : 4 * q + 4, :].bitcast(I32),
+            )
+        load_tab(0)
+
+        w4_codes = keep("w4_codes", [P, PASSES * 2 * K], U8)
+        w4_planes = keep("w4_planes", [P, PASSES * K], U8)
+        nc.vector.tensor_copy(
+            out=w4_codes[:].bitcast(U16).rearrange("p (g t q) -> p g t q", t=PACK, q=P),
+            in_=w4_raw[:].bitcast(U16).rearrange("p (g q t) -> p g t q", t=PACK, q=P),
+        )
+        w4_planes_raw = keep("w4_planes_raw", [P, PASSES * K], U8, "slot_w4")
+        nc.vector.memset(w4_planes_raw[:].bitcast(I32), 0)
+        for q in range(4):
+            nc.sync.dma_start(
+                out=w4_planes_raw[32 * q : 32 * q + 4, :].bitcast(I32).rearrange("r (a c) -> r a c", a=PASSES),
+                in_=w4_scales[:, 4 * q : 4 * q + 4, :].bitcast(I32).rearrange("a r c -> r a c"),
+            )
+        v_planes = keep("v_planes", [P, S], U8)
+        v2_planes = keep("v2_planes", [P, S2], U8)
+
+        v_codes = {}
+        v2_codes = {}
+
+        def gather_v(a, jh):
+            v_codes[a, jh] = keep("v_codes%d%d" % (a, jh), [P, NJ], U32)
+            cols = slice(jh * NJ // 16, (jh + 1) * NJ // 16)
+            nc.vector.tensor_copy(v_codes[a, jh][:], tab[a][:].bitcast(U32).indirect(list1[:, cols]))
+
+        def gather_v2(a):
+            v2_codes[a] = keep("v2_codes%d" % a, [P, S2], U32)
+            nc.vector.tensor_copy(v2_codes[a][:], tab[a][:].bitcast(U32).indirect(list2[:]))
+
+        w1_grouped = {}
+        w1_codes = {}
+        w1_planes = {}
+
+        def round_w1(a, b, on_scalar):
+            w1_grouped[a, b] = keep("w1_grouped%d%d" % (a, b), [P, PASS * PACK], BF16, "slot_grouped%d%d" % (a, b))
+            dst = w1_grouped[a, b][:].rearrange("p (t q j) -> p q t j", t=PACK, j=PACK)
+            src = w1_raw[a, b][:].rearrange("p j (q t) -> p q t j", t=PACK)
+            if on_scalar:
+                nc.scalar.copy(out=dst, in_=src)
+            else:
+                nc.vector.tensor_copy(out=dst, in_=src)
+
+        def quantize_w1(a, b):
+            w1_codes[a, b] = keep("w1_codes%d%d" % (a, b), [P, PASS], U32)
+            w1_planes[a, b] = keep("w1_planes%d%d" % (a, b), [P, PASS], U8)
+            nc.vector.quantize_mx(
+                out=w1_codes[a, b][:].bitcast(FP8X4), scales=w1_planes[a, b][:], in_=w1_grouped[a, b][:]
+            )
+
+        def bank(n):
+            return psum.tile([P, NJ], F32, name="bank%d" % n)
+
+        def v_plane(a, jh):
+            tile = v_planes if a == 0 else v_planes_hi
+            return tile[:, NJ * jh : NJ * (jh + 1)]
+
+        def pass_w4(acc, a, b, t, jh, start):
+            col = (a * PASSES + b) * PASS + t * P
+            nc.tensor.matmul_mx(
+                out=acc[:],
+                lhsT=w4_codes[:, 2 * col : 2 * (col + P)].bitcast(FP4X4),
+                lhsT_scale=w4_planes[:, col : col + P],
+                rhs=v_codes[a, jh][:].bitcast(FP8X4),
+                rhs_scale=v_plane(a, jh),
+                start=start,
+                stop=False,
+            )
+
+        def pass_w1(acc, a, b, t, jh, start, stop):
+            nc.tensor.matmul_mx(
+                out=acc[:],
+                lhsT=w1_codes[a, b][:, t * P : (t + 1) * P].bitcast(FP8X4),
+                lhsT_scale=w1_planes[a, b][:, t * P : (t + 1) * P],
+                rhs=v_codes[a, jh][:].bitcast(FP8X4),
+                rhs_scale=v_plane(a, jh),
+                start=start,
+                stop=stop,
+            )
+
+        def detuning(b, jh, first_bank):
+            accs = [bank(first_bank + t) for t in range(PACK)]
+            if jh == 0:
+                for t in range(PACK):
+                    pass_w1(accs[t], 0, b, t, jh, True, False)
+                    pass_w4(accs[t], 0, b, t, jh, False)
+                for t in range(PACK):
+                    pass_w4(accs[t], 1, b, t, jh, False)
+                    pass_w1(accs[t], 1, b, t, jh, False, True)
+            else:
+                for t in range(PACK):
+                    pass_w1(accs[t], 0, b, t, jh, True, False)
+                    pass_w4(accs[t], 0, b, t, jh, False)
+                    pass_w4(accs[t], 1, b, t, jh, False)
+                    pass_w1(accs[t], 1, b, t, jh, False, True)
+            return accs
+
+        def closeness(accs):
+            close = ring.tile([P, PACK, NJ], F32, name="close")
+            sizes = [keep("size%d" % u, [P, 2, NJ], F32, "slot_size%d" % u) for u in range(2)]
+            for t in range(PACK):
+                nc.scalar.activation(sizes[t // 2][:, t % 2, :], accs[t][:], ACT.Abs)
+                if t >= 2:
+                    u = t - 2
+                    nc.scalar.activation(close[:, 2 * u : 2 * u + 2, :], sizes[u][:], ACT.Exp, scale=-1.0)
+            return close
+
+        h_codes = {}
+        h_planes = {}
+
+        def quantize_h(b, jh, close):
+            grouped = keep("h_grouped", [P, NJ * PACK], BF16, "slot_h%d" % b)
+            nc.vector.tensor_tensor(
+                grouped[:].rearrange("p (c i t) -> p c t i", i=4, t=PACK),
+                close[:].rearrange("p t (c i) -> p c t i", i=4),
+                gains[:, b, :].unsqueeze(1).unsqueeze(3).to_broadcast([P, NJ // 4, PACK, 4]),
+                ALU.mult,
+            )
+            h_codes[b, jh] = keep("h_codes%d%d" % (b, jh), [P, NJ], U32)
+            h_planes[b, jh] = keep("h_planes%d%d" % (b, jh), [P, NJ], U8)
+            nc.vector.quantize_mx(out=h_codes[b, jh][:].bitcast(FP8X4), scales=h_planes[b, jh][:], in_=grouped[:])
+
+        def pair_phases(jh, first_bank):
+            accs = [bank(first_bank + m) for m in range(MT)]
+            for b in range(PASSES):
+                for m in range(MT):
+                    nc.tensor.matmul_mx(
+                        out=accs[m][:],
+                        lhsT=v2_codes[b][:, m * P : (m + 1) * P].bitcast(FP8X4),
+                        lhsT_scale=v2_planes[4 * b :, m * P : (m + 1) * P],
+                        rhs=h_codes[b, jh][:].bitcast(FP8X4),
+                        rhs_scale=h_planes[b, jh][:],
+                        start=(b == 0),
+                        stop=(b == PASSES - 1),
+                    )
+            return accs
+
+        def reduce_turns(jh, accs):
+            rest = keep("rest%d" % jh, [P, MT, NJ], F32)
+            turns = [ring.tile([P, NJ], I32, name="turns", bufs=4) for m in range(MT)]
+            for step in range(MT + 1):
+                if step < MT:
+                    nc.vector.tensor_scalar(
+                        turns[step][:], accs[step][:], shifts[:, step : step + 1], 1.0 / TWO_PI, ALU.add, ALU.mult
+                    )
+                if step > 0:
+                    m = step - 1
+                    nc.vector.scalar_tensor_tensor(
+                        rest[:, m, :], turns[m][:], -TWO_PI, accs[m][:], ALU.mult, ALU.add
+                    )
+            return rest
+
+        def finish(jh, rest):
+            cols = slice(NJ * jh, NJ * (jh + 1))
+            beat = keep("beat%d" % jh, [P, MT, NJ], F32, ("slot_size1", "slot_beat")[jh])
+            score = keep("score%d" % jh, [P, MT, NJ], F32, ("slot_h1", "slot_score")[jh])
+            engine = (nc.gpsimd, nc.vector)[jh]
+            for m in range(MT):
+                nc.scalar.activation(beat[:, m, :], rest[:, m, :], ACT.Sin, bias=shifts[:, m : m + 1])
+                engine.tensor_tensor(score[:, m, :], beat[:, m, :], losses[:, m, cols], ALU.mult)
+                nc.sync.dma_start(out=out[m * P : (m + 1) * P, cols], in_=score[:, m, :])
+
+        round_w1(0, 0, True)
+        load_tab(1)
+        round_w1(1, 0, True)
+        gains = keep("gains", [P, PASSES, PACK], F32, "slot_w10")
+        nc.sync.dma_start(out=gains[:], in_=gain.rearrange("(b p t) -> p b t", b=PASSES, t=PACK))
+        nc.vector.tensor_copy(v_planes[:], tab_planes[:].indirect(list1[:]))
+        nc.scalar.dma_start(out=v_planes_hi[0:112, :].bitcast(I32), in_=v_planes[4:116, :].bitcast(I32))
+        quantize_w1(0, 0)
+        nc.vector.tensor_copy(v2_planes[:], tab_planes[:].indirect(list2[:]))
+        load_w1(0, 1)
+        quantize_w1(1, 0)
+        gather_v(0, 0)
+        nc.vector.tensor_copy(
+            out=w4_planes[:].rearrange("p (g t q) -> p g t q", t=PACK, q=P),
+            in_=w4_planes_raw[:].rearrange("p (g q t) -> p g t q", t=PACK, q=P),
+        )
+        load_w1(1, 1)
+        phases = keep("phases", [P, MT], F32, "slot_grouped10")
+        with nc.allow_non_contiguous_dma(reason="one value to a partition and tile of rows"):
+            nc.sync.dma_start(out=phases[:], in_=phase.rearrange("(m p) -> p m", p=P))
+        gather_v(0, 1)
+        gather_v2(0)
+        losses = keep("losses", [P, MT, S], F32, "slot_tab0")
+        nc.sync.dma_start(out=losses[:], in_=loss.rearrange("(m p) j -> p m j", p=P))
+        gather_v(1, 0)
+        x00 = detuning(0, 0, 0)
+        c00 = closeness(x00)
+        round_w1(0, 1, False)
+        quantize_w1(0, 1)
+        gather_v(1, 1)
+        round_w1(1, 1, False)
+        quantize_w1(1, 1)
+        gather_v2(1)
+        shifts = keep("shifts", [P, MT], F32)
+        nc.vector.tensor_scalar_add(shifts[:], phases[:], 0.5 * math.pi)
+        x10 = detuning(1, 0, 4)
+        quantize_h(0, 0, c00)
+        c10 = closeness(x10)
+        x01 = detuning(0, 1, 0)
+        quantize_h(1, 0, c10)
+        c01 = closeness(x01)
+        x11 = detuning(1, 1, 4)
+        e0 = pair_phases(0, 0)
+        r0 = reduce_turns(0, e0)
+        quantize_h(0, 1, c01)
+        c11 = closeness(x11)
+        quantize_h(1, 1, c11)
+        e1 = pair_phases(1, 4)
+        r1 = reduce_turns(1, e1)
+        finish(0, r0)
+        finish(1, r1)

@@ -178,21 +178,28 @@ def tile_list_beat_disturbance_scores_kernel(
             sizes = [keep("size%d" % u, [P, 2, NJ], F32, "slot_size%d" % u) for u in range(2)]
             for t in range(PACK):
                 nc.scalar.activation(sizes[t // 2][:, t % 2, :], accs[t][:], ACT.Abs)
-                if t >= 2:
-                    u = t - 2
-                    nc.scalar.activation(close[:, 2 * u : 2 * u + 2, :], sizes[u][:], ACT.Exp, scale=-1.0)
+            for u in range(2):
+                nc.scalar.activation(close[:, 2 * u : 2 * u + 2, :], sizes[u][:], ACT.Exp, scale=-1.0)
             return close
 
         h_codes = {}
         h_planes = {}
 
-        def quantize_h(b, jh, close):
+        def apply_gain(b, close, engine):
+            scaled = ring.tile([P, PACK, NJ], BF16, name="scaled")
+            for t in range(PACK):
+                factor = gains[:, b, t : t + 1]
+                if engine is nc.scalar:
+                    nc.scalar.activation(scaled[:, t, :], close[:, t, :], ACT.Copy, scale=factor)
+                else:
+                    engine.tensor_scalar(scaled[:, t, :], close[:, t, :], factor, 0.0, ALU.mult, ALU.add)
+            return scaled
+
+        def quantize_h(b, jh, scaled):
             grouped = keep("h_grouped", [P, NJ * PACK], BF16, "slot_h%d" % b)
-            nc.vector.tensor_tensor(
-                grouped[:].rearrange("p (c i t) -> p c t i", i=4, t=PACK),
-                close[:].rearrange("p t (c i) -> p c t i", i=4),
-                gains[:, b, :].unsqueeze(1).unsqueeze(3).to_broadcast([P, NJ // 4, PACK, 4]),
-                ALU.mult,
+            nc.vector.tensor_copy(
+                out=grouped[:].rearrange("p (c i t) -> p c t i", i=4, t=PACK),
+                in_=scaled[:].rearrange("p t (c i) -> p c t i", i=4),
             )
             h_codes[b, jh] = keep("h_codes%d%d" % (b, jh), [P, NJ], U32)
             h_planes[b, jh] = keep("h_planes%d%d" % (b, jh), [P, NJ], U8)
@@ -232,8 +239,8 @@ def tile_list_beat_disturbance_scores_kernel(
             cols = slice(NJ * jh, NJ * (jh + 1))
             beat = keep("beat%d" % jh, [P, MT, NJ], F32, ("slot_size1", "slot_beat")[jh])
             score = keep("score%d" % jh, [P, MT, NJ], F32, ("slot_h1", "slot_score")[jh])
-            engine = (nc.gpsimd, nc.vector)[jh]
             for m in range(MT):
+                engine = nc.gpsimd if jh * MT + m <= MT else nc.vector
                 nc.scalar.activation(beat[:, m, :], rest[:, m, :], ACT.Sin, bias=shifts[:, m : m + 1])
                 engine.tensor_tensor(score[:, m, :], beat[:, m, :], losses[:, m, cols], ALU.mult)
                 nc.sync.dma_start(out=out[m * P : (m + 1) * P, cols], in_=score[:, m, :])
@@ -274,17 +281,18 @@ def tile_list_beat_disturbance_scores_kernel(
         shifts = keep("shifts", [P, MT], F32)
         nc.vector.tensor_scalar_add(shifts[:], phases[:], 0.5 * math.pi)
         x10 = detuning(1, 0, 4)
-        quantize_h(0, 0, c00)
+        quantize_h(0, 0, apply_gain(0, c00, nc.vector))
         c10 = closeness(x10)
         x01 = detuning(0, 1, 0)
-        quantize_h(1, 0, c10)
+        quantize_h(1, 0, apply_gain(1, c10, nc.vector))
         c01 = closeness(x01)
+        s01 = apply_gain(0, c01, nc.gpsimd)
         x11 = detuning(1, 1, 4)
         e0 = pair_phases(0, 0)
         r0 = reduce_turns(0, e0)
-        quantize_h(0, 1, c01)
+        quantize_h(0, 1, s01)
         c11 = closeness(x11)
-        quantize_h(1, 1, c11)
+        quantize_h(1, 1, apply_gain(1, c11, nc.scalar))
         e1 = pair_phases(1, 4)
         r1 = reduce_turns(1, e1)
         finish(0, r0)

@@ -25,7 +25,7 @@ NJ = 512
 HALVES = S // NJ
 MT = S2 // P
 TWO_PI = 2.0 * math.pi
-W1_SLOT = {(0, 0): "slot_w00", (1, 0): "slot_w10", (0, 1): "slot_w01", (1, 1): "slot_w4"}
+W1_SLOT = {(0, 0): "slot_w00", (1, 0): "slot_w10", (0, 1): "slot_w10", (1, 1): "slot_grouped10"}
 
 
 def tile_list_beat_disturbance_scores_kernel(
@@ -40,13 +40,14 @@ def tile_list_beat_disturbance_scores_kernel(
         def keep(name, shape, dtype, tag=None):
             return held.tile(shape, dtype, name=name, tag=tag or name, align_bytes=64)
 
-        tab_planes = keep("tab_planes", [P, T], U8, "slot_w01")
-        v_planes_hi = keep("v_planes_hi", [P, S], U8)
-        warm = keep("warm", [P, 16], F32, "slot_tab0")
-        nc.vector.memset(warm[:, 0:8], 0.0)
+        tab_planes = keep("tab_planes", [P, T], U8, "slot_gain")
+        picked_hi = keep("picked_hi", [P, S + S2], U8)
+        warm_in = keep("warm_in", [P, 1], F32, "slot_tab0")
+        warm_out = keep("warm_out", [P, 1], F32, "slot_w10")
+        nc.vector.memset(warm_in[:], 0.0)
         nc.vector.memset(tab_planes[:].bitcast(I32), 0)
-        nc.vector.memset(v_planes_hi[:].bitcast(I32), 0)
-        nc.scalar.activation(warm[:, 8:9], warm[:, 0:1], ACT.Exp)
+        nc.vector.memset(picked_hi[:].bitcast(I32), 0)
+        nc.scalar.activation(warm_out[:], warm_in[:], ACT.Exp)
 
         list1 = keep("list1", [P, S // 16], U16)
         list2 = keep("list2", [P, S2 // 16], U16)
@@ -69,13 +70,13 @@ def tile_list_beat_disturbance_scores_kernel(
             in_=w4_words.bitcast(I32).rearrange("a p c -> p a c"),
         )
         load_w1(0, 0)
-        load_w1(1, 0)
         nc.sync.dma_start(list2[:], offs2)
-        for q in range(4):
+        for r in range(4):
             nc.scalar.dma_start(
-                out=tab_planes[32 * q : 32 * q + 8, :].bitcast(I32),
-                in_=tab_scales[:, 4 * q : 4 * q + 4, :].bitcast(I32),
+                out=tab_planes[r:P:16, :].bitcast(I32),
+                in_=tab_scales[:, r:16:4, :].bitcast(I32).rearrange("a q c -> q a c"),
             )
+        load_w1(1, 0)
         load_tab(0)
 
         w4_codes = keep("w4_codes", [P, PASSES * 2 * K], U8)
@@ -91,19 +92,18 @@ def tile_list_beat_disturbance_scores_kernel(
                 out=w4_planes_raw[32 * q : 32 * q + 4, :].bitcast(I32).rearrange("r (a c) -> r a c", a=PASSES),
                 in_=w4_scales[:, 4 * q : 4 * q + 4, :].bitcast(I32).rearrange("a r c -> r a c"),
             )
-        v_planes = keep("v_planes", [P, S], U8)
-        v2_planes = keep("v2_planes", [P, S2], U8)
+        picked = keep("picked", [P, S + S2], U8)
 
         v_codes = {}
         v2_codes = {}
 
-        def gather_v(a, jh):
-            v_codes[a, jh] = keep("v_codes%d%d" % (a, jh), [P, NJ], U32)
+        def gather_v(a, jh, tile=None):
+            v_codes[a, jh] = keep("v_codes%d%d" % (a, jh), [P, NJ], U32)[:] if tile is None else tile
             cols = slice(jh * NJ // 16, (jh + 1) * NJ // 16)
             nc.vector.tensor_copy(v_codes[a, jh][:], tab[a][:].bitcast(U32).indirect(list1[:, cols]))
 
-        def gather_v2(a):
-            v2_codes[a] = keep("v2_codes%d" % a, [P, S2], U32)
+        def gather_v2(a, tile=None):
+            v2_codes[a] = keep("v2_codes%d" % a, [P, S2], U32)[:] if tile is None else tile
             nc.vector.tensor_copy(v2_codes[a][:], tab[a][:].bitcast(U32).indirect(list2[:]))
 
         w1_grouped = {}
@@ -112,8 +112,8 @@ def tile_list_beat_disturbance_scores_kernel(
 
         def round_w1(a, b, on_scalar):
             w1_grouped[a, b] = keep("w1_grouped%d%d" % (a, b), [P, PASS * PACK], BF16, "slot_grouped%d%d" % (a, b))
-            dst = w1_grouped[a, b][:].rearrange("p (t q j) -> p q t j", t=PACK, j=PACK)
-            src = w1_raw[a, b][:].rearrange("p j (q t) -> p q t j", t=PACK)
+            dst = w1_grouped[a, b][:].rearrange("p (t q j) -> p q j t", t=PACK, j=PACK)
+            src = w1_raw[a, b][:].rearrange("p j (q t) -> p q j t", t=PACK)
             if on_scalar:
                 nc.scalar.copy(out=dst, in_=src)
             else:
@@ -130,8 +130,7 @@ def tile_list_beat_disturbance_scores_kernel(
             return psum.tile([P, NJ], F32, name="bank%d" % n)
 
         def v_plane(a, jh):
-            tile = v_planes if a == 0 else v_planes_hi
-            return tile[:, NJ * jh : NJ * (jh + 1)]
+            return (picked, picked_hi)[a][:, NJ * jh : NJ * (jh + 1)]
 
         def pass_w4(acc, a, b, t, jh, start):
             col = (a * PASSES + b) * PASS + t * P
@@ -145,7 +144,7 @@ def tile_list_beat_disturbance_scores_kernel(
                 stop=False,
             )
 
-        def pass_w1(acc, a, b, t, jh, start, stop):
+        def pass_w1(acc, a, b, t, jh, stop, start=False):
             nc.tensor.matmul_mx(
                 out=acc[:],
                 lhsT=w1_codes[a, b][:, t * P : (t + 1) * P].bitcast(FP8X4),
@@ -156,38 +155,43 @@ def tile_list_beat_disturbance_scores_kernel(
                 stop=stop,
             )
 
-        def detuning(b, jh, first_bank):
-            accs = [bank(first_bank + t) for t in range(PACK)]
-            if jh == 0:
-                for t in range(PACK):
-                    pass_w1(accs[t], 0, b, t, jh, True, False)
-                    pass_w4(accs[t], 0, b, t, jh, False)
-                for t in range(PACK):
-                    pass_w4(accs[t], 1, b, t, jh, False)
-                    pass_w1(accs[t], 1, b, t, jh, False, True)
-            else:
-                for t in range(PACK):
-                    pass_w1(accs[t], 0, b, t, jh, True, False)
-                    pass_w4(accs[t], 0, b, t, jh, False)
-                    pass_w4(accs[t], 1, b, t, jh, False)
-                    pass_w1(accs[t], 1, b, t, jh, False, True)
-            return accs
+        def banks(first_bank):
+            return [bank(first_bank + n) for n in range(4)]
 
-        def closeness(accs):
+        def detuning(acc, b, t, jh):
+            pass_w4(acc, 0, b, t, jh, True)
+            pass_w1(acc, 0, b, t, jh, False)
+            pass_w4(acc, 1, b, t, jh, False)
+            pass_w1(acc, 1, b, t, jh, True)
+
+        def closeness(accs, early_exp):
             close = ring.tile([P, PACK, NJ], F32, name="close")
             sizes = [keep("size%d" % u, [P, 2, NJ], F32, "slot_size%d" % u) for u in range(2)]
-            for t in range(PACK):
+
+            def absolute(t):
                 nc.scalar.activation(sizes[t // 2][:, t % 2, :], accs[t][:], ACT.Abs)
-            for u in range(2):
+
+            def exponential(u):
                 nc.scalar.activation(close[:, 2 * u : 2 * u + 2, :], sizes[u][:], ACT.Exp, scale=-1.0)
+
+            absolute(0)
+            absolute(1)
+            absolute(2)
+            if early_exp:
+                exponential(0)
+                absolute(3)
+            else:
+                absolute(3)
+                exponential(0)
+            exponential(1)
             return close
 
         h_codes = {}
         h_planes = {}
 
-        def apply_gain(b, close, engine):
+        def apply_gain(b, close, engines):
             scaled = ring.tile([P, PACK, NJ], BF16, name="scaled")
-            for t in range(PACK):
+            for t, engine in enumerate(engines):
                 factor = gains[:, b, t : t + 1]
                 if engine is nc.scalar:
                     nc.scalar.activation(scaled[:, t, :], close[:, t, :], ACT.Copy, scale=factor)
@@ -197,28 +201,32 @@ def tile_list_beat_disturbance_scores_kernel(
 
         def quantize_h(b, jh, scaled):
             grouped = keep("h_grouped", [P, NJ * PACK], BF16, "slot_h%d" % b)
-            nc.vector.tensor_copy(
-                out=grouped[:].rearrange("p (c i t) -> p c t i", i=4, t=PACK),
-                in_=scaled[:].rearrange("p t (c i) -> p c t i", i=4),
-            )
             h_codes[b, jh] = keep("h_codes%d%d" % (b, jh), [P, NJ], U32)
             h_planes[b, jh] = keep("h_planes%d%d" % (b, jh), [P, NJ], U8)
-            nc.vector.quantize_mx(out=h_codes[b, jh][:].bitcast(FP8X4), scales=h_planes[b, jh][:], in_=grouped[:])
+            halves = [slice(u * NJ // 2, (u + 1) * NJ // 2) for u in range(2)]
+            by_column = grouped[:].rearrange("p (n t) -> p n t", t=PACK)
+            for cols in halves:
+                nc.vector.tensor_copy(
+                    out=by_column[:, cols, :].rearrange("p (c i) t -> p c t i", i=4),
+                    in_=scaled[:, :, cols].rearrange("p t (c i) -> p c t i", i=4),
+                )
+            for cols in halves:
+                nc.vector.quantize_mx(
+                    out=h_codes[b, jh][:, cols].bitcast(FP8X4),
+                    scales=h_planes[b, jh][:, cols],
+                    in_=by_column[:, cols, :].rearrange("p n t -> p (n t)"),
+                )
 
-        def pair_phases(jh, first_bank):
-            accs = [bank(first_bank + m) for m in range(MT)]
-            for b in range(PASSES):
-                for m in range(MT):
-                    nc.tensor.matmul_mx(
-                        out=accs[m][:],
-                        lhsT=v2_codes[b][:, m * P : (m + 1) * P].bitcast(FP8X4),
-                        lhsT_scale=v2_planes[4 * b :, m * P : (m + 1) * P],
-                        rhs=h_codes[b, jh][:].bitcast(FP8X4),
-                        rhs_scale=h_planes[b, jh][:],
-                        start=(b == 0),
-                        stop=(b == PASSES - 1),
-                    )
-            return accs
+        def pass_pairs(acc, b, m, jh):
+            nc.tensor.matmul_mx(
+                out=acc[:],
+                lhsT=v2_codes[b][:, m * P : (m + 1) * P].bitcast(FP8X4),
+                lhsT_scale=(picked, picked_hi)[b][:, S + m * P : S + (m + 1) * P],
+                rhs=h_codes[b, jh][:].bitcast(FP8X4),
+                rhs_scale=h_planes[b, jh][:],
+                start=(b == 0),
+                stop=(b == PASSES - 1),
+            )
 
         def reduce_turns(jh, accs):
             rest = keep("rest%d" % jh, [P, MT, NJ], F32)
@@ -248,52 +256,77 @@ def tile_list_beat_disturbance_scores_kernel(
         round_w1(0, 0, True)
         load_tab(1)
         round_w1(1, 0, True)
-        gains = keep("gains", [P, PASSES, PACK], F32, "slot_w10")
-        nc.sync.dma_start(out=gains[:], in_=gain.rearrange("(b p t) -> p b t", b=PASSES, t=PACK))
-        nc.vector.tensor_copy(v_planes[:], tab_planes[:].indirect(list1[:]))
-        nc.scalar.dma_start(out=v_planes_hi[0:112, :].bitcast(I32), in_=v_planes[4:116, :].bitcast(I32))
-        quantize_w1(0, 0)
-        nc.vector.tensor_copy(v2_planes[:], tab_planes[:].indirect(list2[:]))
         load_w1(0, 1)
+        nc.vector.tensor_copy(picked[:, 0:S], tab_planes[:].indirect(list1[:]))
+        nc.vector.tensor_copy(picked[:, S:], tab_planes[:].indirect(list2[:]))
+        nc.scalar.dma_start(out=picked_hi[0 : P - 16, :].bitcast(I32), in_=picked[16:P, :].bitcast(I32))
+        gains = keep("gains", [P, PASSES, PACK], F32, "slot_gain")
+        nc.sync.dma_start(out=gains[:], in_=gain.rearrange("(b p t) -> p b t", b=PASSES, t=PACK))
+        quantize_w1(0, 0)
+        phases = keep("phases", [P, MT], F32, "slot_grouped00")
+        with nc.allow_non_contiguous_dma(reason="one value to a partition and tile of rows"):
+            nc.sync.dma_start(out=phases[:], in_=phase.rearrange("(m p) -> p m", p=P))
         quantize_w1(1, 0)
+        load_w1(1, 1)
         gather_v(0, 0)
         nc.vector.tensor_copy(
             out=w4_planes[:].rearrange("p (g t q) -> p g t q", t=PACK, q=P),
             in_=w4_planes_raw[:].rearrange("p (g q t) -> p g t q", t=PACK, q=P),
         )
-        load_w1(1, 1)
-        phases = keep("phases", [P, MT], F32, "slot_grouped10")
-        with nc.allow_non_contiguous_dma(reason="one value to a partition and tile of rows"):
-            nc.sync.dma_start(out=phases[:], in_=phase.rearrange("(m p) -> p m", p=P))
-        gather_v(0, 1)
-        gather_v2(0)
+        later_codes = keep("later_codes", [P, NJ + S2], U32, "slot_w4")
+        gather_v(0, 1, later_codes[:, 0:NJ])
+        gather_v2(0, later_codes[:, NJ:])
         losses = keep("losses", [P, MT, S], F32, "slot_tab0")
         nc.sync.dma_start(out=losses[:], in_=loss.rearrange("(m p) j -> p m j", p=P))
+        x00 = banks(0)
+        x10 = banks(4)
+        for t in range(PACK):
+            pass_w1(x00[t], 0, 0, t, 0, False, True)
+        for t in range(PACK):
+            pass_w4(x00[t], 0, 0, t, 0, False)
+        for t in range(PACK):
+            pass_w4(x10[t], 0, 1, t, 0, True)
         gather_v(1, 0)
-        x00 = detuning(0, 0, 0)
-        c00 = closeness(x00)
+        for t in range(PACK):
+            pass_w4(x00[t], 1, 0, t, 0, False)
+            pass_w1(x00[t], 1, 0, t, 0, True)
+        c00 = closeness(x00, False)
+        for t in range(PACK):
+            pass_w4(x10[t], 1, 1, t, 0, False)
         round_w1(0, 1, False)
         quantize_w1(0, 1)
-        gather_v(1, 1)
+        for t in range(PACK):
+            pass_w1(x10[t], 0, 1, t, 0, False)
         round_w1(1, 1, False)
         quantize_w1(1, 1)
+        for t in range(PACK):
+            pass_w1(x10[t], 1, 1, t, 0, True)
+        gather_v(1, 1)
         gather_v2(1)
         shifts = keep("shifts", [P, MT], F32)
         nc.vector.tensor_scalar_add(shifts[:], phases[:], 0.5 * math.pi)
-        x10 = detuning(1, 0, 4)
-        quantize_h(0, 0, apply_gain(0, c00, nc.vector))
-        c10 = closeness(x10)
-        x01 = detuning(0, 1, 0)
-        quantize_h(1, 0, apply_gain(1, c10, nc.vector))
-        c01 = closeness(x01)
-        s01 = apply_gain(0, c01, nc.gpsimd)
-        x11 = detuning(1, 1, 4)
-        e0 = pair_phases(0, 0)
+        quantize_h(0, 0, apply_gain(0, c00, [nc.vector] * PACK))
+        c10 = closeness(x10, False)
+        x01 = banks(0)
+        for t in range(PACK):
+            detuning(x01[t], 0, t, 1)
+        quantize_h(1, 0, apply_gain(1, c10, [nc.vector] * PACK))
+        c01 = closeness(x01, False)
+        s01 = apply_gain(0, c01, [nc.gpsimd] * PACK)
+        x11 = banks(4)
+        e0 = banks(0)
+        for n in range(4):
+            detuning(x11[n], 1, n, 1)
+            for b in range(PASSES):
+                pass_pairs(e0[n], b, n, 0)
         r0 = reduce_turns(0, e0)
         quantize_h(0, 1, s01)
-        c11 = closeness(x11)
-        quantize_h(1, 1, apply_gain(1, c11, nc.scalar))
-        e1 = pair_phases(1, 4)
+        c11 = closeness(x11, True)
+        quantize_h(1, 1, apply_gain(1, c11, [nc.scalar, nc.scalar, nc.vector, nc.vector]))
+        e1 = banks(4)
+        for b in range(PASSES):
+            for m in range(MT):
+                pass_pairs(e1[m], b, m, 1)
         r1 = reduce_turns(1, e1)
         finish(0, r0)
         finish(1, r1)

@@ -22,10 +22,19 @@ PACK = 4
 PASS = P * PACK
 PASSES = K // PASS
 NJ = 512
-HALVES = S // NJ
+NU = 128
+UNITS = S // NU
+UNITS_PER_HALF = NJ // NU
+PAIRS = UNITS // 2
+CLOSE_SLOTS = 4
 MT = S2 // P
+QUADRANTS = 4
+ROWS = 4
+SECOND_PASS_ROW = 16
+COLUMN_HALVES = (slice(0, NJ // 2), slice(NJ // 2, NJ))
+WHOLE = slice(0, NJ)
+GPSIMD_TILES = 5
 TWO_PI = 2.0 * math.pi
-W1_SLOT = {(0, 0): "slot_w00", (1, 0): "slot_w10", (0, 1): "slot_w10", (1, 1): "slot_grouped10"}
 
 
 def tile_list_beat_disturbance_scores_kernel(
@@ -34,19 +43,18 @@ def tile_list_beat_disturbance_scores_kernel(
     nc = tc.nc
     with ExitStack() as ctx:
         held = ctx.enter_context(tc.tile_pool(name="held", bufs=1))
-        ring = ctx.enter_context(tc.tile_pool(name="ring", bufs=2))
         psum = ctx.enter_context(tc.psum_pool(name="psum", bufs=1))
 
-        def keep(name, shape, dtype, tag=None):
-            return held.tile(shape, dtype, name=name, tag=tag or name, align_bytes=64)
+        def keep(name, shape, dtype, slot=None):
+            return held.tile(shape, dtype, name=name, tag=slot or name, align_bytes=64)
 
-        tab_planes = keep("tab_planes", [P, T], U8, "slot_gain")
-        picked_hi = keep("picked_hi", [P, S + S2], U8)
+        tab_planes = keep("tab_planes", [P, T], U8, "slot_planes_w01")
+        picked_second = keep("picked_second", [P, S + S2], U8)
         warm_in = keep("warm_in", [P, 1], F32, "slot_tab0")
         warm_out = keep("warm_out", [P, 1], F32, "slot_w10")
         nc.vector.memset(warm_in[:], 0.0)
         nc.vector.memset(tab_planes[:].bitcast(I32), 0)
-        nc.vector.memset(picked_hi[:].bitcast(I32), 0)
+        nc.vector.memset(picked_second[:].bitcast(I32), 0)
         nc.scalar.activation(warm_out[:], warm_in[:], ACT.Exp)
 
         list1 = keep("list1", [P, S // 16], U16)
@@ -55,29 +63,29 @@ def tile_list_beat_disturbance_scores_kernel(
         tab = {}
         w1_raw = {}
 
-        def load_tab(a):
-            tab[a] = keep("tab%d" % a, [P, T], I32, ("slot_tab0", "slot_w00")[a])
+        def load_tab(a, slot):
+            tab[a] = keep("tab%d" % a, [P, T], I32, slot)
             nc.sync.dma_start(out=tab[a][:], in_=tab_words[a].rearrange("p t i -> p (t i)").bitcast(I32))
 
-        def load_w1(a, b):
-            w1_raw[a, b] = keep("w1_raw%d%d" % (a, b), [P, PACK, PASS], F32, W1_SLOT[a, b])
+        def load_w1(a, b, slot):
+            w1_raw[a, b] = keep("w1_raw%d%d" % (a, b), [P, PACK, PASS], F32, slot)
             rows = w1[PASS * a : PASS * (a + 1), PASS * b : PASS * (b + 1)]
-            nc.sync.dma_start(out=w1_raw[a, b][:], in_=rows.rearrange("(p j) c -> p j c", j=PACK))
+            nc.sync.dma_start(out=w1_raw[a, b][:], in_=rows.rearrange("(p i) c -> p i c", i=PACK))
 
         nc.sync.dma_start(list1[:], offs)
         nc.sync.dma_start(
             out=w4_raw[:].bitcast(I32).rearrange("p (a c) -> p a c", a=PASSES),
             in_=w4_words.bitcast(I32).rearrange("a p c -> p a c"),
         )
-        load_w1(0, 0)
+        load_w1(0, 0, "slot_w00")
         nc.sync.dma_start(list2[:], offs2)
-        for r in range(4):
+        for s in range(ROWS):
             nc.scalar.dma_start(
-                out=tab_planes[r:P:16, :].bitcast(I32),
-                in_=tab_scales[:, r:16:4, :].bitcast(I32).rearrange("a q c -> q a c"),
+                out=tab_planes[s:P:SECOND_PASS_ROW, :].bitcast(I32),
+                in_=tab_scales[:, s : QUADRANTS * ROWS : ROWS, :].bitcast(I32).rearrange("a q c -> q a c"),
             )
-        load_w1(1, 0)
-        load_tab(0)
+        load_w1(1, 0, "slot_w10")
+        load_tab(0, "slot_tab0")
 
         w4_codes = keep("w4_codes", [P, PASSES * 2 * K], U8)
         w4_planes = keep("w4_planes", [P, PASSES * K], U8)
@@ -87,37 +95,36 @@ def tile_list_beat_disturbance_scores_kernel(
         )
         w4_planes_raw = keep("w4_planes_raw", [P, PASSES * K], U8, "slot_w4")
         nc.vector.memset(w4_planes_raw[:].bitcast(I32), 0)
-        for q in range(4):
+        for quad in range(QUADRANTS):
             nc.sync.dma_start(
-                out=w4_planes_raw[32 * q : 32 * q + 4, :].bitcast(I32).rearrange("r (a c) -> r a c", a=PASSES),
-                in_=w4_scales[:, 4 * q : 4 * q + 4, :].bitcast(I32).rearrange("a r c -> r a c"),
+                out=w4_planes_raw[32 * quad : 32 * quad + ROWS, :].bitcast(I32).rearrange("s (a c) -> s a c", a=PASSES),
+                in_=w4_scales[:, ROWS * quad : ROWS * (quad + 1), :].bitcast(I32).rearrange("a s c -> s a c"),
             )
-        picked = keep("picked", [P, S + S2], U8)
+        picked_first = keep("picked_first", [P, S + S2], U8)
+        picked_planes = (picked_first, picked_second)
 
         v_codes = {}
         v2_codes = {}
 
-        def gather_v(a, jh, tile=None):
-            v_codes[a, jh] = keep("v_codes%d%d" % (a, jh), [P, NJ], U32)[:] if tile is None else tile
-            cols = slice(jh * NJ // 16, (jh + 1) * NJ // 16)
-            nc.vector.tensor_copy(v_codes[a, jh][:], tab[a][:].bitcast(U32).indirect(list1[:, cols]))
+        def gather_v(a, jh, codes):
+            v_codes[a, jh] = codes
+            entries = slice(jh * NJ // 16, (jh + 1) * NJ // 16)
+            nc.vector.tensor_copy(codes, tab[a][:].bitcast(U32).indirect(list1[:, entries]))
 
-        def gather_v2(a, tile=None):
-            v2_codes[a] = keep("v2_codes%d" % a, [P, S2], U32)[:] if tile is None else tile
-            nc.vector.tensor_copy(v2_codes[a][:], tab[a][:].bitcast(U32).indirect(list2[:]))
+        def gather_v2(a, codes):
+            v2_codes[a] = codes
+            nc.vector.tensor_copy(codes, tab[a][:].bitcast(U32).indirect(list2[:]))
 
         w1_grouped = {}
         w1_codes = {}
         w1_planes = {}
 
-        def round_w1(a, b, on_scalar):
+        def round_w1(a, b, copy):
             w1_grouped[a, b] = keep("w1_grouped%d%d" % (a, b), [P, PASS * PACK], BF16, "slot_grouped%d%d" % (a, b))
-            dst = w1_grouped[a, b][:].rearrange("p (t q j) -> p q j t", t=PACK, j=PACK)
-            src = w1_raw[a, b][:].rearrange("p j (q t) -> p q j t", t=PACK)
-            if on_scalar:
-                nc.scalar.copy(out=dst, in_=src)
-            else:
-                nc.vector.tensor_copy(out=dst, in_=src)
+            copy(
+                out=w1_grouped[a, b][:].rearrange("p (t q i) -> p q i t", t=PACK, i=PACK),
+                in_=w1_raw[a, b][:].rearrange("p i (q t) -> p q i t", t=PACK),
+            )
 
         def quantize_w1(a, b):
             w1_codes[a, b] = keep("w1_codes%d%d" % (a, b), [P, PASS], U32)
@@ -126,149 +133,138 @@ def tile_list_beat_disturbance_scores_kernel(
                 out=w1_codes[a, b][:].bitcast(FP8X4), scales=w1_planes[a, b][:], in_=w1_grouped[a, b][:]
             )
 
-        def bank(n):
-            return psum.tile([P, NJ], F32, name="bank%d" % n)
+        def unit_banks():
+            return [psum.tile([P, PACK, NU], F32, name="bank%d" % c) for c in range(UNITS)]
 
-        def v_plane(a, jh):
-            return (picked, picked_hi)[a][:, NJ * jh : NJ * (jh + 1)]
+        def unit_passes(acc, weights, a, c, start, stop):
+            jh, n0 = divmod(c * NU, NJ)
+            for t, (codes, plane) in enumerate(weights):
+                nc.tensor.matmul_mx(
+                    out=acc[:, t, :],
+                    lhsT=codes,
+                    lhsT_scale=plane,
+                    rhs=v_codes[a, jh][:, n0 : n0 + NU].bitcast(FP8X4),
+                    rhs_scale=picked_planes[a][:, c * NU : (c + 1) * NU],
+                    start=start and t == 0,
+                    stop=stop and t == PACK - 1,
+                )
 
-        def pass_w4(acc, a, b, t, jh, start):
-            col = (a * PASSES + b) * PASS + t * P
-            nc.tensor.matmul_mx(
-                out=acc[:],
-                lhsT=w4_codes[:, 2 * col : 2 * (col + P)].bitcast(FP4X4),
-                lhsT_scale=w4_planes[:, col : col + P],
-                rhs=v_codes[a, jh][:].bitcast(FP8X4),
-                rhs_scale=v_plane(a, jh),
-                start=start,
-                stop=False,
+        def passes_w4(acc, a, b, c, start=False):
+            firsts = [(a * PASSES + b) * PASS + t * P for t in range(PACK)]
+            weights = [
+                (w4_codes[:, 2 * col : 2 * (col + P)].bitcast(FP4X4), w4_planes[:, col : col + P]) for col in firsts
+            ]
+            unit_passes(acc, weights, a, c, start, False)
+
+        def passes_w1(acc, a, b, c, start=False, stop=False):
+            slices = [slice(t * P, (t + 1) * P) for t in range(PACK)]
+            weights = [(w1_codes[a, b][:, cols].bitcast(FP8X4), w1_planes[a, b][:, cols]) for cols in slices]
+            unit_passes(acc, weights, a, c, start, stop)
+
+        sizes = {}
+        closes = {}
+
+        def absolute(acc, b, c):
+            u = b * PAIRS + c // 2
+            if c % 2 == 0:
+                sizes[u] = keep("size%d" % u, [P, 2, NU, PACK], F32, "slot_size%d" % (u % 2))
+            nc.scalar.activation(sizes[u][:, c % 2, :, :], acc[:].rearrange("p t n -> p n t"), ACT.Abs)
+
+        def exponential(u):
+            closes[u] = keep("close%d" % u, [P, 2 * NU, PACK], F32, "slot_close%d" % (u % CLOSE_SLOTS))
+            nc.scalar.activation(
+                closes[u][:].rearrange("p n t -> p (n t)"),
+                sizes[u][:].rearrange("p c n t -> p (c n t)"),
+                ACT.Exp,
+                scale=-1.0,
             )
-
-        def pass_w1(acc, a, b, t, jh, stop, start=False):
-            nc.tensor.matmul_mx(
-                out=acc[:],
-                lhsT=w1_codes[a, b][:, t * P : (t + 1) * P].bitcast(FP8X4),
-                lhsT_scale=w1_planes[a, b][:, t * P : (t + 1) * P],
-                rhs=v_codes[a, jh][:].bitcast(FP8X4),
-                rhs_scale=v_plane(a, jh),
-                start=start,
-                stop=stop,
-            )
-
-        def banks(first_bank):
-            return [bank(first_bank + n) for n in range(4)]
-
-        def detuning(acc, b, t, jh):
-            pass_w4(acc, 0, b, t, jh, True)
-            pass_w1(acc, 0, b, t, jh, False)
-            pass_w4(acc, 1, b, t, jh, False)
-            pass_w1(acc, 1, b, t, jh, True)
-
-        def closeness(accs, early_exp):
-            close = ring.tile([P, PACK, NJ], F32, name="close")
-            sizes = [keep("size%d" % u, [P, 2, NJ], F32, "slot_size%d" % u) for u in range(2)]
-
-            def absolute(t):
-                nc.scalar.activation(sizes[t // 2][:, t % 2, :], accs[t][:], ACT.Abs)
-
-            def exponential(u):
-                nc.scalar.activation(close[:, 2 * u : 2 * u + 2, :], sizes[u][:], ACT.Exp, scale=-1.0)
-
-            absolute(0)
-            absolute(1)
-            absolute(2)
-            if early_exp:
-                exponential(0)
-                absolute(3)
-            else:
-                absolute(3)
-                exponential(0)
-            exponential(1)
-            return close
 
         h_codes = {}
         h_planes = {}
 
-        def apply_gain(b, close, engines):
-            scaled = ring.tile([P, PACK, NJ], BF16, name="scaled")
-            for t, engine in enumerate(engines):
-                factor = gains[:, b, t : t + 1]
-                if engine is nc.scalar:
-                    nc.scalar.activation(scaled[:, t, :], close[:, t, :], ACT.Copy, scale=factor)
-                else:
-                    engine.tensor_scalar(scaled[:, t, :], close[:, t, :], factor, 0.0, ALU.mult, ALU.add)
-            return scaled
-
-        def quantize_h(b, jh, scaled):
-            grouped = keep("h_grouped", [P, NJ * PACK], BF16, "slot_h%d" % b)
-            h_codes[b, jh] = keep("h_codes%d%d" % (b, jh), [P, NJ], U32)
-            h_planes[b, jh] = keep("h_planes%d%d" % (b, jh), [P, NJ], U8)
-            halves = [slice(u * NJ // 2, (u + 1) * NJ // 2) for u in range(2)]
-            by_column = grouped[:].rearrange("p (n t) -> p n t", t=PACK)
-            for cols in halves:
-                nc.vector.tensor_copy(
-                    out=by_column[:, cols, :].rearrange("p (c i) t -> p c t i", i=4),
-                    in_=scaled[:, :, cols].rearrange("p t (c i) -> p c t i", i=4),
-                )
-            for cols in halves:
+        def round_and_quantize_h(u):
+            b, i = divmod(u, PAIRS)
+            jh, n0 = divmod(2 * NU * i, NJ)
+            if n0 == 0:
+                h_codes[b, jh] = keep("h_codes%d%d" % (b, jh), [P, NJ], U32)
+                h_planes[b, jh] = keep("h_planes%d%d" % (b, jh), [P, NJ], U8)
+            rounded = keep("h_rounded%d" % u, [P, 2 * NU, PACK], BF16, "slot_h%d" % (u % 2))
+            factors = gains[:, b, :].unsqueeze(1).to_broadcast([P, NU, PACK])
+            for n in (0, NU):
+                nc.vector.tensor_tensor(rounded[:, n : n + NU, :], closes[u][:, n : n + NU, :], factors, ALU.mult)
+            for n in (0, NU):
                 nc.vector.quantize_mx(
-                    out=h_codes[b, jh][:, cols].bitcast(FP8X4),
-                    scales=h_planes[b, jh][:, cols],
-                    in_=by_column[:, cols, :].rearrange("p n t -> p (n t)"),
+                    out=h_codes[b, jh][:, n0 + n : n0 + n + NU].bitcast(FP8X4),
+                    scales=h_planes[b, jh][:, n0 + n : n0 + n + NU],
+                    in_=rounded[:, n : n + NU, :].rearrange("p n t -> p (n t)"),
                 )
 
-        def pass_pairs(acc, b, m, jh):
-            nc.tensor.matmul_mx(
-                out=acc[:],
-                lhsT=v2_codes[b][:, m * P : (m + 1) * P].bitcast(FP8X4),
-                lhsT_scale=(picked, picked_hi)[b][:, S + m * P : S + (m + 1) * P],
-                rhs=h_codes[b, jh][:].bitcast(FP8X4),
-                rhs_scale=h_planes[b, jh][:],
-                start=(b == 0),
-                stop=(b == PASSES - 1),
-            )
+        def pair_phases(jh, order):
+            accs = [psum.tile([P, NJ], F32, name="bank%d" % (MT * jh + m)) for m in range(MT)]
+            for b, m in order:
+                nc.tensor.matmul_mx(
+                    out=accs[m][:],
+                    lhsT=v2_codes[b][:, m * P : (m + 1) * P].bitcast(FP8X4),
+                    lhsT_scale=picked_planes[b][:, S + m * P : S + (m + 1) * P],
+                    rhs=h_codes[b, jh][:].bitcast(FP8X4),
+                    rhs_scale=h_planes[b, jh][:],
+                    start=(b == 0),
+                    stop=(b == PASSES - 1),
+                )
+            return accs
 
-        def reduce_turns(jh, accs):
+        def pieces(jh):
+            whole = [(m, WHOLE) for m in range(MT)]
+            if jh == 0:
+                return whole
+            return whole[:-1] + [(MT - 1, cols) for cols in COLUMN_HALVES]
+
+        def reduce_turns(jh, accs, turns_slot):
             rest = keep("rest%d" % jh, [P, MT, NJ], F32)
-            turns = [ring.tile([P, NJ], I32, name="turns", bufs=4) for m in range(MT)]
-            for step in range(MT + 1):
-                if step < MT:
+            turns = keep("turns%d" % jh, [P, MT, NJ], I32, turns_slot)
+            todo = pieces(jh)
+            for step in range(len(todo) + 1):
+                if step < len(todo):
+                    m, cols = todo[step]
                     nc.vector.tensor_scalar(
-                        turns[step][:], accs[step][:], shifts[:, step : step + 1], 1.0 / TWO_PI, ALU.add, ALU.mult
+                        turns[:, m, cols], accs[m][:, cols], shifts[:, m : m + 1], 1.0 / TWO_PI, ALU.add, ALU.mult
                     )
                 if step > 0:
-                    m = step - 1
+                    m, cols = todo[step - 1]
                     nc.vector.scalar_tensor_tensor(
-                        rest[:, m, :], turns[m][:], -TWO_PI, accs[m][:], ALU.mult, ALU.add
+                        rest[:, m, cols], turns[:, m, cols], -TWO_PI, accs[m][:, cols], ALU.mult, ALU.add
                     )
             return rest
 
-        def finish(jh, rest):
-            cols = slice(NJ * jh, NJ * (jh + 1))
-            beat = keep("beat%d" % jh, [P, MT, NJ], F32, ("slot_size1", "slot_beat")[jh])
-            score = keep("score%d" % jh, [P, MT, NJ], F32, ("slot_h1", "slot_score")[jh])
-            for m in range(MT):
-                engine = nc.gpsimd if jh * MT + m <= MT else nc.vector
-                nc.scalar.activation(beat[:, m, :], rest[:, m, :], ACT.Sin, bias=shifts[:, m : m + 1])
-                engine.tensor_tensor(score[:, m, :], beat[:, m, :], losses[:, m, cols], ALU.mult)
-                nc.sync.dma_start(out=out[m * P : (m + 1) * P, cols], in_=score[:, m, :])
+        def finish(jh, rest, beat_slot, score_slot):
+            beat = keep("beat%d" % jh, [P, MT, NJ], F32, beat_slot)
+            score = keep("score%d" % jh, [P, MT, NJ], F32, score_slot)
+            for m, cols in pieces(jh):
+                engine = nc.gpsimd if jh * MT + m < GPSIMD_TILES else nc.vector
+                j = slice(NJ * jh + cols.start, NJ * jh + cols.stop)
+                nc.scalar.activation(beat[:, m, cols], rest[:, m, cols], ACT.Sin, bias=shifts[:, m : m + 1])
+                engine.tensor_tensor(score[:, m, cols], beat[:, m, cols], losses[:, m, j], ALU.mult)
+                nc.sync.dma_start(out=out[m * P : (m + 1) * P, j], in_=score[:, m, cols])
 
-        round_w1(0, 0, True)
-        load_tab(1)
-        round_w1(1, 0, True)
-        load_w1(0, 1)
-        nc.vector.tensor_copy(picked[:, 0:S], tab_planes[:].indirect(list1[:]))
-        nc.vector.tensor_copy(picked[:, S:], tab_planes[:].indirect(list2[:]))
-        nc.scalar.dma_start(out=picked_hi[0 : P - 16, :].bitcast(I32), in_=picked[16:P, :].bitcast(I32))
-        gains = keep("gains", [P, PASSES, PACK], F32, "slot_gain")
-        nc.sync.dma_start(out=gains[:], in_=gain.rearrange("(b p t) -> p b t", b=PASSES, t=PACK))
+        round_w1(0, 0, nc.scalar.copy)
+        load_tab(1, "slot_w00")
+        round_w1(1, 0, nc.scalar.copy)
+        nc.vector.tensor_copy(picked_first[:, 0:S], tab_planes[:].indirect(list1[:]))
+        nc.vector.tensor_copy(picked_first[:, S:], tab_planes[:].indirect(list2[:]))
+        nc.sync.dma_start(
+            out=picked_second[0 : P - SECOND_PASS_ROW, :].bitcast(I32),
+            in_=picked_first[SECOND_PASS_ROW:P, :].bitcast(I32),
+        )
+        load_w1(0, 1, "slot_planes_w01")
         quantize_w1(0, 0)
-        phases = keep("phases", [P, MT], F32, "slot_grouped00")
-        with nc.allow_non_contiguous_dma(reason="one value to a partition and tile of rows"):
-            nc.sync.dma_start(out=phases[:], in_=phase.rearrange("(m p) -> p m", p=P))
+        load_w1(1, 1, "slot_grouped00")
+        gains = keep("gains", [P, PASSES, PACK], F32, "slot_w10")
+        nc.sync.dma_start(out=gains[:], in_=gain.rearrange("(b p t) -> p b t", b=PASSES, t=PACK))
         quantize_w1(1, 0)
-        load_w1(1, 1)
-        gather_v(0, 0)
+        phases = keep("phases", [P, MT], F32, "slot_grouped10")
+        with nc.allow_non_contiguous_dma(reason="one value for each partition and tile of rows"):
+            nc.sync.dma_start(out=phases[:], in_=phase.rearrange("(m p) -> p m", p=P))
+        gather_v(0, 0, keep("v_codes00", [P, NJ], U32)[:])
         nc.vector.tensor_copy(
             out=w4_planes[:].rearrange("p (g t q) -> p g t q", t=PACK, q=P),
             in_=w4_planes_raw[:].rearrange("p (g q t) -> p g t q", t=PACK, q=P),
@@ -278,55 +274,58 @@ def tile_list_beat_disturbance_scores_kernel(
         gather_v2(0, later_codes[:, NJ:])
         losses = keep("losses", [P, MT, S], F32, "slot_tab0")
         nc.sync.dma_start(out=losses[:], in_=loss.rearrange("(m p) j -> p m j", p=P))
-        x00 = banks(0)
-        x10 = banks(4)
-        for t in range(PACK):
-            pass_w1(x00[t], 0, 0, t, 0, False, True)
-        for t in range(PACK):
-            pass_w4(x00[t], 0, 0, t, 0, False)
-        for t in range(PACK):
-            pass_w4(x10[t], 0, 1, t, 0, True)
-        gather_v(1, 0)
-        for t in range(PACK):
-            pass_w4(x00[t], 1, 0, t, 0, False)
-            pass_w1(x00[t], 1, 0, t, 0, True)
-        c00 = closeness(x00, False)
-        for t in range(PACK):
-            pass_w4(x10[t], 1, 1, t, 0, False)
-        round_w1(0, 1, False)
-        quantize_w1(0, 1)
-        for t in range(PACK):
-            pass_w1(x10[t], 0, 1, t, 0, False)
-        round_w1(1, 1, False)
-        quantize_w1(1, 1)
-        for t in range(PACK):
-            pass_w1(x10[t], 1, 1, t, 0, True)
-        gather_v(1, 1)
-        gather_v2(1)
+
+        first_half = range(UNITS_PER_HALF)
+        second_half = range(UNITS_PER_HALF, UNITS)
+        x0 = unit_banks()
+        for c in first_half:
+            passes_w1(x0[c], 0, 0, c, start=True)
+        for c in first_half:
+            passes_w4(x0[c], 0, 0, c)
+        for c in second_half:
+            passes_w1(x0[c], 0, 0, c, start=True)
+        gather_v(1, 0, keep("v_codes10", [P, NJ], U32)[:])
+        for c in first_half:
+            passes_w4(x0[c], 1, 0, c)
+            passes_w1(x0[c], 1, 0, c, stop=True)
+        gather_v(1, 1, keep("v_codes11", [P, NJ], U32)[:])
+        for c in second_half:
+            passes_w4(x0[c], 1, 0, c)
+            passes_w4(x0[c], 0, 0, c)
+            passes_w1(x0[c], 1, 0, c, stop=True)
+        for a in range(PASSES):
+            round_w1(a, 1, nc.vector.tensor_copy)
+            quantize_w1(a, 1)
+        gather_v2(1, keep("v2_codes1", [P, S2], U32)[:])
         shifts = keep("shifts", [P, MT], F32)
         nc.vector.tensor_scalar_add(shifts[:], phases[:], 0.5 * math.pi)
-        quantize_h(0, 0, apply_gain(0, c00, [nc.vector] * PACK))
-        c10 = closeness(x10, False)
-        x01 = banks(0)
-        for t in range(PACK):
-            detuning(x01[t], 0, t, 1)
-        quantize_h(1, 0, apply_gain(1, c10, [nc.vector] * PACK))
-        c01 = closeness(x01, False)
-        s01 = apply_gain(0, c01, [nc.gpsimd] * PACK)
-        x11 = banks(4)
-        e0 = banks(0)
-        for n in range(4):
-            detuning(x11[n], 1, n, 1)
-            for b in range(PASSES):
-                pass_pairs(e0[n], b, n, 0)
-        r0 = reduce_turns(0, e0)
-        quantize_h(0, 1, s01)
-        c11 = closeness(x11, True)
-        quantize_h(1, 1, apply_gain(1, c11, [nc.scalar, nc.scalar, nc.vector, nc.vector]))
-        e1 = banks(4)
-        for b in range(PASSES):
-            for m in range(MT):
-                pass_pairs(e1[m], b, m, 1)
-        r1 = reduce_turns(1, e1)
-        finish(0, r0)
-        finish(1, r1)
+
+        def make_h(u):
+            exponential(u)
+            round_and_quantize_h(u)
+
+        for c in range(UNITS):
+            absolute(x0[c], 0, c)
+            if c % 2 == 0 and c > 0:
+                make_h(c // 2 - 1)
+        x1 = unit_banks()
+        for c in range(UNITS):
+            for a in range(PASSES):
+                passes_w4(x1[c], a, 1, c, start=(a == 0))
+            for a in range(PASSES):
+                passes_w1(x1[c], a, 1, c, stop=(a == PASSES - 1))
+        for c in range(UNITS):
+            absolute(x1[c], 1, c)
+            if c % 2 == 0:
+                make_h(PAIRS + c // 2 - 1)
+        last_pair = PASSES * PAIRS - 1
+        make_h(last_pair)
+
+        by_bank = [(b, m) for m in range(MT) for b in range(PASSES)]
+        by_pass = [(b, m) for b in range(PASSES) for m in range(MT)]
+        turns_slot = "slot_close%d" % ((last_pair - 1) % CLOSE_SLOTS)
+        rest0 = reduce_turns(0, pair_phases(0, by_bank), turns_slot)
+        rest1 = reduce_turns(1, pair_phases(1, by_pass), turns_slot)
+
+        finish(0, rest0, "slot_size%d" % (last_pair % 2), "slot_h%d" % (last_pair % 2))
+        finish(1, rest1, "slot_beat", "slot_score")

import math
from contextlib import ExitStack

import concourse.mybir as mybir

K, T, S, S2 = 1024, 4096, 1024, 512
FLOPS = 2 * (2 * K * K * S + K * S * S2)

F32 = mybir.dt.float32
BF16 = mybir.dt.bfloat16
I32 = mybir.dt.int32
U32 = mybir.dt.uint32
U16 = mybir.dt.uint16
U8 = mybir.dt.uint8
FP8X4 = mybir.dt.float8_e4m3fn_x4
FP4X4 = mybir.dt.float4_e2m1fn_x4
ALU = mybir.AluOpType
ACT = mybir.ActivationFunctionType

P = 128
PACK = 4
PASS = P * PACK
PASSES = K // PASS
NJ = 512
NU = 128
UNITS = S // NU
UNITS_PER_HALF = NJ // NU
PAIRS = UNITS // 2
CLOSE_SLOTS = 4
MT = S2 // P
QUADRANTS = 4
ROWS = 4
SECOND_PASS_ROW = 16
COLUMN_HALVES = (slice(0, NJ // 2), slice(NJ // 2, NJ))
WHOLE = slice(0, NJ)
GPSIMD_TILES = 5
TWO_PI = 2.0 * math.pi


def tile_list_beat_disturbance_scores_kernel(
    tc, tab_words, tab_scales, offs, offs2, w4_words, w4_scales, w1, gain, phase, loss, out
):
    nc = tc.nc
    with ExitStack() as ctx:
        held = ctx.enter_context(tc.tile_pool(name="held", bufs=1))
        psum = ctx.enter_context(tc.psum_pool(name="psum", bufs=1))

        def keep(name, shape, dtype, slot=None):
            return held.tile(shape, dtype, name=name, tag=slot or name, align_bytes=64)

        tab_planes = keep("tab_planes", [P, T], U8, "slot_planes_w01")
        picked_second = keep("picked_second", [P, S + S2], U8)
        warm_in = keep("warm_in", [P, 1], F32, "slot_tab0")
        warm_out = keep("warm_out", [P, 1], F32, "slot_w10")
        nc.vector.memset(warm_in[:], 0.0)
        nc.vector.memset(tab_planes[:].bitcast(I32), 0)
        nc.vector.memset(picked_second[:].bitcast(I32), 0)
        nc.scalar.activation(warm_out[:], warm_in[:], ACT.Exp)

        list1 = keep("list1", [P, S // 16], U16)
        list2 = keep("list2", [P, S2 // 16], U16)
        w4_raw = keep("w4_raw", [P, PASSES * 2 * K], U8, "slot_w4")
        tab = {}
        w1_raw = {}

        def load_tab(a, slot):
            tab[a] = keep("tab%d" % a, [P, T], I32, slot)
            nc.sync.dma_start(out=tab[a][:], in_=tab_words[a].rearrange("p t i -> p (t i)").bitcast(I32))

        def load_w1(a, b, slot):
            w1_raw[a, b] = keep("w1_raw%d%d" % (a, b), [P, PACK, PASS], F32, slot)
            rows = w1[PASS * a : PASS * (a + 1), PASS * b : PASS * (b + 1)]
            nc.sync.dma_start(out=w1_raw[a, b][:], in_=rows.rearrange("(p i) c -> p i c", i=PACK))

        nc.sync.dma_start(list1[:], offs)
        nc.sync.dma_start(
            out=w4_raw[:].bitcast(I32).rearrange("p (a c) -> p a c", a=PASSES),
            in_=w4_words.bitcast(I32).rearrange("a p c -> p a c"),
        )
        load_w1(0, 0, "slot_w00")
        nc.sync.dma_start(list2[:], offs2)
        for s in range(ROWS):
            nc.scalar.dma_start(
                out=tab_planes[s:P:SECOND_PASS_ROW, :].bitcast(I32),
                in_=tab_scales[:, s : QUADRANTS * ROWS : ROWS, :].bitcast(I32).rearrange("a q c -> q a c"),
            )
        load_w1(1, 0, "slot_w10")
        load_tab(0, "slot_tab0")

        w4_codes = keep("w4_codes", [P, PASSES * 2 * K], U8)
        w4_planes = keep("w4_planes", [P, PASSES * K], U8)
        nc.vector.tensor_copy(
            out=w4_codes[:].bitcast(U16).rearrange("p (g t q) -> p g t q", t=PACK, q=P),
            in_=w4_raw[:].bitcast(U16).rearrange("p (g q t) -> p g t q", t=PACK, q=P),
        )
        w4_planes_raw = keep("w4_planes_raw", [P, PASSES * K], U8, "slot_w4")
        nc.vector.memset(w4_planes_raw[:].bitcast(I32), 0)
        for quad in range(QUADRANTS):
            nc.sync.dma_start(
                out=w4_planes_raw[32 * quad : 32 * quad + ROWS, :].bitcast(I32).rearrange("s (a c) -> s a c", a=PASSES),
                in_=w4_scales[:, ROWS * quad : ROWS * (quad + 1), :].bitcast(I32).rearrange("a s c -> s a c"),
            )
        picked_first = keep("picked_first", [P, S + S2], U8)
        picked_planes = (picked_first, picked_second)

        v_codes = {}
        v2_codes = {}

        def gather_v(a, jh, codes):
            v_codes[a, jh] = codes
            entries = slice(jh * NJ // 16, (jh + 1) * NJ // 16)
            nc.vector.tensor_copy(codes, tab[a][:].bitcast(U32).indirect(list1[:, entries]))

        def gather_v2(a, codes):
            v2_codes[a] = codes
            nc.vector.tensor_copy(codes, tab[a][:].bitcast(U32).indirect(list2[:]))

        w1_grouped = {}
        w1_codes = {}
        w1_planes = {}

        def round_w1(a, b, copy):
            w1_grouped[a, b] = keep("w1_grouped%d%d" % (a, b), [P, PASS * PACK], BF16, "slot_grouped%d%d" % (a, b))
            copy(
                out=w1_grouped[a, b][:].rearrange("p (t q i) -> p q i t", t=PACK, i=PACK),
                in_=w1_raw[a, b][:].rearrange("p i (q t) -> p q i t", t=PACK),
            )

        def quantize_w1(a, b):
            w1_codes[a, b] = keep("w1_codes%d%d" % (a, b), [P, PASS], U32)
            w1_planes[a, b] = keep("w1_planes%d%d" % (a, b), [P, PASS], U8)
            nc.vector.quantize_mx(
                out=w1_codes[a, b][:].bitcast(FP8X4), scales=w1_planes[a, b][:], in_=w1_grouped[a, b][:]
            )

        def unit_banks():
            return [psum.tile([P, PACK, NU], F32, name="bank%d" % c) for c in range(UNITS)]

        def unit_passes(acc, weights, a, c, start, stop):
            jh, n0 = divmod(c * NU, NJ)
            for t, (codes, plane) in enumerate(weights):
                nc.tensor.matmul_mx(
                    out=acc[:, t, :],
                    lhsT=codes,
                    lhsT_scale=plane,
                    rhs=v_codes[a, jh][:, n0 : n0 + NU].bitcast(FP8X4),
                    rhs_scale=picked_planes[a][:, c * NU : (c + 1) * NU],
                    start=start and t == 0,
                    stop=stop and t == PACK - 1,
                )

        def passes_w4(acc, a, b, c, start=False):
            firsts = [(a * PASSES + b) * PASS + t * P for t in range(PACK)]
            weights = [
                (w4_codes[:, 2 * col : 2 * (col + P)].bitcast(FP4X4), w4_planes[:, col : col + P]) for col in firsts
            ]
            unit_passes(acc, weights, a, c, start, False)

        def passes_w1(acc, a, b, c, start=False, stop=False):
            slices = [slice(t * P, (t + 1) * P) for t in range(PACK)]
            weights = [(w1_codes[a, b][:, cols].bitcast(FP8X4), w1_planes[a, b][:, cols]) for cols in slices]
            unit_passes(acc, weights, a, c, start, stop)

        sizes = {}
        closes = {}

        def absolute(acc, b, c):
            u = b * PAIRS + c // 2
            if c % 2 == 0:
                sizes[u] = keep("size%d" % u, [P, 2, NU, PACK], F32, "slot_size%d" % (u % 2))
            nc.scalar.activation(sizes[u][:, c % 2, :, :], acc[:].rearrange("p t n -> p n t"), ACT.Abs)

        def exponential(u):
            closes[u] = keep("close%d" % u, [P, 2 * NU, PACK], F32, "slot_close%d" % (u % CLOSE_SLOTS))
            nc.scalar.activation(
                closes[u][:].rearrange("p n t -> p (n t)"),
                sizes[u][:].rearrange("p c n t -> p (c n t)"),
                ACT.Exp,
                scale=-1.0,
            )

        h_codes = {}
        h_planes = {}

        def round_and_quantize_h(u):
            b, i = divmod(u, PAIRS)
            jh, n0 = divmod(2 * NU * i, NJ)
            if n0 == 0:
                h_codes[b, jh] = keep("h_codes%d%d" % (b, jh), [P, NJ], U32)
                h_planes[b, jh] = keep("h_planes%d%d" % (b, jh), [P, NJ], U8)
            rounded = keep("h_rounded%d" % u, [P, 2 * NU, PACK], BF16, "slot_h%d" % (u % 2))
            factors = gains[:, b, :].unsqueeze(1).to_broadcast([P, NU, PACK])
            for n in (0, NU):
                nc.vector.tensor_tensor(rounded[:, n : n + NU, :], closes[u][:, n : n + NU, :], factors, ALU.mult)
            for n in (0, NU):
                nc.vector.quantize_mx(
                    out=h_codes[b, jh][:, n0 + n : n0 + n + NU].bitcast(FP8X4),
                    scales=h_planes[b, jh][:, n0 + n : n0 + n + NU],
                    in_=rounded[:, n : n + NU, :].rearrange("p n t -> p (n t)"),
                )

        def pair_phases(jh, order):
            accs = [psum.tile([P, NJ], F32, name="bank%d" % (MT * jh + m)) for m in range(MT)]
            for b, m in order:
                nc.tensor.matmul_mx(
                    out=accs[m][:],
                    lhsT=v2_codes[b][:, m * P : (m + 1) * P].bitcast(FP8X4),
                    lhsT_scale=picked_planes[b][:, S + m * P : S + (m + 1) * P],
                    rhs=h_codes[b, jh][:].bitcast(FP8X4),
                    rhs_scale=h_planes[b, jh][:],
                    start=(b == 0),
                    stop=(b == PASSES - 1),
                )
            return accs

        def pieces(jh):
            whole = [(m, WHOLE) for m in range(MT)]
            if jh == 0:
                return whole
            return whole[:-1] + [(MT - 1, cols) for cols in COLUMN_HALVES]

        def reduce_turns(jh, accs, turns_slot):
            rest = keep("rest%d" % jh, [P, MT, NJ], F32)
            turns = keep("turns%d" % jh, [P, MT, NJ], I32, turns_slot)
            todo = pieces(jh)
            for step in range(len(todo) + 1):
                if step < len(todo):
                    m, cols = todo[step]
                    nc.vector.tensor_scalar(
                        turns[:, m, cols], accs[m][:, cols], shifts[:, m : m + 1], 1.0 / TWO_PI, ALU.add, ALU.mult
                    )
                if step > 0:
                    m, cols = todo[step - 1]
                    nc.vector.scalar_tensor_tensor(
                        rest[:, m, cols], turns[:, m, cols], -TWO_PI, accs[m][:, cols], ALU.mult, ALU.add
                    )
            return rest

        def finish(jh, rest, beat_slot, score_slot):
            beat = keep("beat%d" % jh, [P, MT, NJ], F32, beat_slot)
            score = keep("score%d" % jh, [P, MT, NJ], F32, score_slot)
            for m, cols in pieces(jh):
                engine = nc.gpsimd if jh * MT + m < GPSIMD_TILES else nc.vector
                j = slice(NJ * jh + cols.start, NJ * jh + cols.stop)
                nc.scalar.activation(beat[:, m, cols], rest[:, m, cols], ACT.Sin, bias=shifts[:, m : m + 1])
                engine.tensor_tensor(score[:, m, cols], beat[:, m, cols], losses[:, m, j], ALU.mult)
                nc.sync.dma_start(out=out[m * P : (m + 1) * P, j], in_=score[:, m, cols])

        round_w1(0, 0, nc.scalar.copy)
        load_tab(1, "slot_w00")
        round_w1(1, 0, nc.scalar.copy)
        nc.vector.tensor_copy(picked_first[:, 0:S], tab_planes[:].indirect(list1[:]))
        nc.vector.tensor_copy(picked_first[:, S:], tab_planes[:].indirect(list2[:]))
        nc.sync.dma_start(
            out=picked_second[0 : P - SECOND_PASS_ROW, :].bitcast(I32),
            in_=picked_first[SECOND_PASS_ROW:P, :].bitcast(I32),
        )
        load_w1(0, 1, "slot_planes_w01")
        quantize_w1(0, 0)
        load_w1(1, 1, "slot_grouped00")
        gains = keep("gains", [P, PASSES, PACK], F32, "slot_w10")
        nc.sync.dma_start(out=gains[:], in_=gain.rearrange("(b p t) -> p b t", b=PASSES, t=PACK))
        quantize_w1(1, 0)
        phases = keep("phases", [P, MT], F32, "slot_grouped10")
        with nc.allow_non_contiguous_dma(reason="one value for each partition and tile of rows"):
            nc.sync.dma_start(out=phases[:], in_=phase.rearrange("(m p) -> p m", p=P))
        gather_v(0, 0, keep("v_codes00", [P, NJ], U32)[:])
        nc.vector.tensor_copy(
            out=w4_planes[:].rearrange("p (g t q) -> p g t q", t=PACK, q=P),
            in_=w4_planes_raw[:].rearrange("p (g q t) -> p g t q", t=PACK, q=P),
        )
        later_codes = keep("later_codes", [P, NJ + S2], U32, "slot_w4")
        gather_v(0, 1, later_codes[:, 0:NJ])
        gather_v2(0, later_codes[:, NJ:])
        losses = keep("losses", [P, MT, S], F32, "slot_tab0")
        nc.sync.dma_start(out=losses[:], in_=loss.rearrange("(m p) j -> p m j", p=P))

        first_half = range(UNITS_PER_HALF)
        second_half = range(UNITS_PER_HALF, UNITS)
        x0 = unit_banks()
        for c in first_half:
            passes_w1(x0[c], 0, 0, c, start=True)
        for c in first_half:
            passes_w4(x0[c], 0, 0, c)
        for c in second_half:
            passes_w1(x0[c], 0, 0, c, start=True)
        gather_v(1, 0, keep("v_codes10", [P, NJ], U32)[:])
        for c in first_half:
            passes_w4(x0[c], 1, 0, c)
            passes_w1(x0[c], 1, 0, c, stop=True)
        gather_v(1, 1, keep("v_codes11", [P, NJ], U32)[:])
        for c in second_half:
            passes_w4(x0[c], 1, 0, c)
            passes_w4(x0[c], 0, 0, c)
            passes_w1(x0[c], 1, 0, c, stop=True)
        for a in range(PASSES):
            round_w1(a, 1, nc.vector.tensor_copy)
            quantize_w1(a, 1)
        gather_v2(1, keep("v2_codes1", [P, S2], U32)[:])
        shifts = keep("shifts", [P, MT], F32)
        nc.vector.tensor_scalar_add(shifts[:], phases[:], 0.5 * math.pi)

        def make_h(u):
            exponential(u)
            round_and_quantize_h(u)

        for c in range(UNITS):
            absolute(x0[c], 0, c)
            if c % 2 == 0 and c > 0:
                make_h(c // 2 - 1)
        x1 = unit_banks()
        for c in range(UNITS):
            for a in range(PASSES):
                passes_w4(x1[c], a, 1, c, start=(a == 0))
            for a in range(PASSES):
                passes_w1(x1[c], a, 1, c, stop=(a == PASSES - 1))
        for c in range(UNITS):
            absolute(x1[c], 1, c)
            if c % 2 == 0:
                make_h(PAIRS + c // 2 - 1)
        last_pair = PASSES * PAIRS - 1
        make_h(last_pair)

        by_bank = [(b, m) for m in range(MT) for b in range(PASSES)]
        by_pass = [(b, m) for b in range(PASSES) for m in range(MT)]
        turns_slot = "slot_close%d" % ((last_pair - 1) % CLOSE_SLOTS)
        rest0 = reduce_turns(0, pair_phases(0, by_bank), turns_slot)
        rest1 = reduce_turns(1, pair_phases(1, by_pass), turns_slot)

        finish(0, rest0, "slot_size%d" % (last_pair % 2), "slot_h%d" % (last_pair % 2))
        finish(1, rest1, "slot_beat", "slot_score")
